import numpy as np, ml_dtypes
CORES = [1,14,19,24,37,42,55,60,65,78,83,88,101,106,119,124]
N = 16
KB, QP = 2, 64
MEM = [7,12]
def setup_inputs(rng):
    q = rng.standard_normal((N, 128, QP), dtype=np.float32) / 4; k = rng.standard_normal((N, 128, KB * 128), dtype=np.float32)
    a = 2 * np.pi * rng.random((N, QP)); s = 400 * rng.random((N, QP)) ** 1.5; q[:, 0, :] = s * np.cos(a); q[:, 1, :] = s * np.sin(a); q[:, 2, :] = 150 * rng.standard_normal((N, QP)); k[:, 2, :] = 1 + k[:, 2, :] / 50
    c = np.zeros(N); c[MEM] = rng.permutation(len(MEM))
    a = (2 * np.pi * rng.random() + np.pi / 2 * (c.reshape(N, 1, 1) + 0.5) / len(MEM) - 0.5 + (np.arange(KB).reshape(1, KB, 1) + rng.random((N, KB, 128))) / KB).reshape(N, KB * 128); k[:, 0, :] = np.cos(a); k[:, 1, :] = np.sin(a)
    return {"q": q.astype(ml_dtypes.bfloat16), "k": k.astype(ml_dtypes.bfloat16), "v": rng.standard_normal((N, 128, KB * 128), dtype=np.float32).astype(ml_dtypes.bfloat16)}
def setup_inputs_big(rng):
    d = setup_inputs(rng)
    for k in ("v",): d[k] = (d[k].astype(np.float32) * 1048576.0).astype(d[k].dtype)
    return d
def setup_inputs_small(rng):
    d = setup_inputs(rng)
    for k in ("v",): d[k] = (d[k].astype(np.float32) * (1 / 1048576.0)).astype(d[k].dtype)
    return d
def reference(q, k, v):
    Q, K, V = q.astype(np.float64), k.astype(np.float64), v.astype(np.float64)
    y = np.zeros((N, QP, 128))
    for r in range(N):
        js = list(MEM)
        S = np.concatenate([K[j].T @ Q[r] for j in js], axis=0)
        P = np.exp(S - S.max(axis=0)); P = P / P.sum(axis=0)
        y[r] = P.T @ np.concatenate([V[j][:, 128 * b:128 * b + 128] for j in js for b in range(KB)], axis=0)
    return {"y": y.astype(ml_dtypes.bfloat16)}

@@ -1,0 +1,226 @@
+import math
+from concourse.bass import DstId, RemoteDMATransfer
+from concourse.mybir import AluOpType, AxisListType, ActivationFunctionType
+
+NQ = 4
+NF = 8
+NR = 8
+NKV = 16
+
+STEP = 64.0
+MAGIC = 12582912.0
+DOWN = math.exp(-STEP)
+
+SCRATCH = {
+    "qs": ("sbuf", [128, 64], "bfloat16"),
+    "qown": ("sbuf", [128, 128], "bfloat16"),
+    "qfar": ("sbuf", [128, 128], "bfloat16"),
+    "kb": ("sbuf", [128, 256], "bfloat16"),
+    "vb": ("sbuf", [128, 256], "bfloat16"),
+    "mask": ("sbuf", [128, 128], "float32"),
+    "ident": ("sbuf", [128, 128], "bfloat16"),
+    "mx": ("sbuf", [128, 4], "float32"),
+    "ls": ("sbuf", [128, 4], "float32"),
+    "p0": ("sbuf", [128, 256], "bfloat16"),
+    "p1": ("sbuf", [128, 256], "bfloat16"),
+    "pt0": ("sbuf", [128, 256], "bfloat16"),
+    "pt1": ("sbuf", [128, 256], "bfloat16"),
+    "res0": ("sbuf", [128, 130], "bfloat16"),
+    "res1": ("sbuf", [128, 130], "bfloat16"),
+    "pa": ("sbuf", [128, 130], "bfloat16"),
+    "pb": ("sbuf", [128, 130], "bfloat16"),
+    "dd": ("sbuf", [128, 1], "float32"),
+    "gg": ("sbuf", [128, 2], "float32"),
+    "aa": ("sbuf", [128, 2], "float32"),
+    "tt": ("sbuf", [128, 129], "float32"),
+    "zz": ("sbuf", [128, 129], "float32"),
+    "rr": ("sbuf", [128, 1], "float32"),
+    "yb": ("sbuf", [128, 128], "bfloat16"),
+    "s0": ("psum", [128, 512], "float32"),
+    "s1": ("psum", [128, 512], "float32"),
+    "o0": ("psum", [128, 512], "float32"),
+    "o1": ("psum", [128, 512], "float32"),
+    "tp00": ("psum", [128, 1024], "bfloat16"),
+    "tp01": ("psum", [128, 1024], "bfloat16"),
+    "tp10": ("psum", [128, 1024], "bfloat16"),
+    "tp11": ("psum", [128, 1024], "bfloat16"),
+}
+
+_BATCH_SEMS = ["sS", "sA", "sB", "sM", "sPa", "sPb", "sTa", "sTb", "sCa", "sCb", "sO", "sL", "sR"]
+SEMAPHORES = (["ql", "kl", "vl", "snt", "qa", "qf", "ka", "va", "res", "i0", "i1", "i2", "st",
+               "c1", "c2", "c3", "c4", "c5", "c6", "c7", "c8", "c9"]
+              + [n + str(b) for b in (0, 1) for n in _BATCH_SEMS])
+
+
+def _engines(topo, src, dsts, n):
+    allowed = topo.mask(src, dsts[0])
+    for d in dsts[1:]:
+        allowed &= topo.mask(src, d)
+    bits = [e for e in range(16) if (allowed >> e) & 1]
+    n = min(n, len(bits))
+    m = 0
+    for e in bits[::len(bits) // n][:n]:
+        m |= 1 << e
+    return m, n
+
+
+def _plan(T, topo):
+    cores = list(T.cores)
+    mem = [cores[j] for j in T.tables["MEM"]]
+    every = range(topo.CHIPS * topo.CORES_PER_CHIP)
+    workers, ranks = [], []
+    for s in (0, 1):
+        ch = topo.chip(mem[s])
+        w = [c for c in every if topo.chip(c) == ch and c not in cores and topo.may_write(c, mem[1 - s])]
+        r = [c for c in cores if topo.chip(c) == ch or topo.same_plane(topo.chip(c), ch)]
+        workers.append({d: [c for c in w if topo.die(c) == d] for d in (0, 1)})
+        ranks.append({d: [c for c in r if topo.die(c) == d] for d in (0, 1)})
+    job = {}
+    home = {}
+    for s in (0, 1):
+        for d in (0, 1):
+            for i, w in enumerate(workers[s][d]):
+                job[w] = (workers[1 - s][d][i], ranks[s][d][2 * i:2 * i + 2], ranks[1 - s][d][2 * i:2 * i + 2])
+                for h, c in enumerate(ranks[s][d][2 * i:2 * i + 2]):
+                    home[c] = (w, h)
+    feeds = {mem[s]: workers[s][0] + workers[s][1] for s in (0, 1)}
+    return job, home, feeds
+
+
+def _q_engines(topo, c, w):
+    return _engines(topo, c, [w], NKV if topo.chip(c) == topo.chip(w) else NQ)
+
+
+def _fan(g, T, topo, core, dsts, src, dst, sem, n):
+    m, n = _engines(topo, core, dsts, n)
+    ids = [DstId(rid=topo.addr(c)[0], pnc=topo.addr(c)[1]) for c in dsts]
+    g.remote_dma_fused([RemoteDMATransfer(dst_ids=ids, dma_engine_mask=m, remote_sem=sem, srcs=[src],
+                                          dsts=[dst for _ in dsts], alu_op=0)], local_sem=T.sem.snt)
+    return n
+
+
+def _worker(g, core, T, topo, job):
+    partner, own, far = job[core]
+    sem = T.sem
+    A, F = AluOpType, ActivationFunctionType
+    te, ve, se = g.tensor, g.vector, g.scalar
+
+    ve.memset(T.mask[:], 0.0).then_inc(sem.i0, 1)
+    g.wait_ge(sem.i0, 1)
+    g.affine_select(T.mask[:], T.mask[:], [[-1, 128]], A.is_equal, -200.0, 0, 1).then_inc(sem.i1, 1)
+    se.wait_ge(sem.i1, 1)
+    se.activation(T.ident[:], T.mask[:], F.Exp).then_inc(sem.i2, 1)
+
+    q_all = sum(_q_engines(topo, c, core)[1] for c in own)
+    g.wait_ge(sem.qa, q_all)
+    m, nf = _engines(topo, core, [partner], NF)
+    rid, pid, _ = topo.addr(partner)
+    g.remote_dma(out_ap=T.qfar[:], in_ap=T.qown[:], remote_sem=sem.qf, local_sem=sem.snt, pid=pid, routing_id=rid,
+                 dma_engine_mask=m)
+    sent = nf
+
+    for b in (0, 1):
+        S = lambda n: sem[n + str(b)]
+        q, s, o, p, pt, res = (T.qown, T.qfar)[b], T["s%d" % b], T["o%d" % b], T["p%d" % b], T["pt%d" % b], T["res%d" % b]
+        tp = [T["tp%d0" % b], T["tp%d1" % b]]
+        mx, kq = T.mx[:, 2 * b:2 * b + 1], T.mx[:, 2 * b + 1:2 * b + 2]
+        nm = res[:, 129:130]
+        if b == 0:
+            te.wait_ge(sem.qa, q_all)
+            te.wait_ge(sem.ka, NKV)
+        else:
+            te.wait_ge(sem.qf, nf)
+        te.matmul(s[:, 0:256], q[:], T.kb[:], True, True).then_inc(S("sS"), 1)
+        ve.wait_ge(S("sS"), 1)
+        ve.tensor_reduce(mx, s[:, 0:256], AxisListType.X, A.max).then_inc(S("sA"), 1)
+        ve.wait_ge(S("sA"), 1)
+        ve.tensor_scalar(kq, mx, 1.0 / STEP, MAGIC, A.mult, A.add).then_inc(S("sB"), 1)
+        ve.wait_ge(S("sB"), 1)
+        ve.tensor_scalar(nm, kq, MAGIC, -STEP, A.subtract, A.mult).then_inc(S("sM"), 1)
+        se.wait_ge(S("sM"), 1)
+        for j, n in enumerate(("sPa", "sPb")):
+            se.activation(p[:, 128 * j:128 * j + 128], s[:, 128 * j:128 * j + 128], F.Exp, bias=nm,
+                          accum_out=T.ls[:, 2 * b + j:2 * b + j + 1]).then_inc(S(n), 1)
+        if b == 0:
+            te.wait_ge(sem.i2, 1)
+        for j, (n, n2) in enumerate((("sPa", "sTa"), ("sPb", "sTb"))):
+            te.wait_ge(S(n), 1)
+            te.transpose(tp[j][:, 0:128], p[:, 128 * j:128 * j + 128], T.ident[:]).then_inc(S(n2), 1)
+        for j, (n, n2) in enumerate((("sTa", "sCa"), ("sTb", "sCb"))):
+            ve.wait_ge(S(n), 1)
+            ve.tensor_copy(pt[:, 128 * j:128 * j + 128], tp[j][:, 0:128]).then_inc(S(n2), 1)
+        if b == 0:
+            te.wait_ge(sem.va, NKV)
+        te.wait_ge(S("sCa"), 1)
+        te.matmul(o[:, 0:128], pt[:, 0:128], T.vb[:, 0:128], True, False)
+        te.wait_ge(S("sCb"), 1)
+        te.matmul(o[:, 0:128], pt[:, 128:256], T.vb[:, 128:256], False, True).then_inc(S("sO"), 1)
+        ve.wait_ge(S("sPa"), 1)
+        ve.wait_ge(S("sPb"), 1)
+        ve.tensor_tensor(res[:, 128:129], T.ls[:, 2 * b:2 * b + 1], T.ls[:, 2 * b + 1:2 * b + 2], A.add).then_inc(S("sL"), 1)
+        ve.wait_ge(S("sO"), 1)
+        ve.tensor_copy(res[:, 0:128], o[:, 0:128]).then_inc(S("sR"), 1)
+        g.wait_ge(S("sM"), 1)
+        g.wait_ge(S("sL"), 1)
+        g.wait_ge(S("sR"), 1)
+        sent += _fan(g, T, topo, core, (own, far)[b], res[:], (T.pa, T.pb)[b][:], sem.res, NR)
+    g.wait_ge(sem.snt, sent)
+
+
+def _rank(g, core, T, topo, job, home, feeds):
+    sem = T.sem
+    A, F = AluOpType, ActivationFunctionType
+    ve, se, sy = g.vector, g.scalar, g.sync
+    w, h = home[core]
+    partner = job[w][0]
+
+    sy.dma_start(T.qs[:], T.q[:]).then_inc(sem.ql, 16)
+    if core in feeds:
+        se.dma_start(T.kb[:], T.k[:]).then_inc(sem.kl, 16)
+        sy.dma_start(T.vb[:], T.v[:]).then_inc(sem.vl, 16)
+    g.wait_ge(sem.ql, 16)
+    m, sent = _q_engines(topo, core, w)
+    rid, pid, _ = topo.addr(w)
+    g.remote_dma(out_ap=T.qown[:, 64 * h:64 * h + 64], in_ap=T.qs[:], remote_sem=sem.qa, local_sem=sem.snt, pid=pid,
+                 routing_id=rid, dma_engine_mask=m)
+    if core in feeds:
+        g.wait_ge(sem.kl, 16)
+        sent += _fan(g, T, topo, core, feeds[core], T.kb[:], T.kb[:], sem.ka, NKV)
+        g.wait_ge(sem.vl, 16)
+        sent += _fan(g, T, topo, core, feeds[core], T.vb[:], T.vb[:], sem.va, NKV)
+    g.wait_ge(sem.snt, sent)
+
+    both = _engines(topo, w, job[w][1], NR)[1] + _engines(topo, partner, job[partner][2], NR)[1]
+    P = slice(64 * h, 64 * h + 64)
+    d = T.dd[P, :]
+    ve.wait_ge(sem.res, both)
+    se.wait_ge(sem.res, both)
+    ve.tensor_tensor(d, T.pb[P, 129:130], T.pa[P, 129:130], A.subtract).then_inc(sem.c1, 1)
+    ve.wait_ge(sem.c1, 1)
+    ve.tensor_scalar(T.gg[P, 1:2], d, STEP, DOWN, A.is_le, A.mult).then_inc(sem.c2, 1)
+    ve.tensor_scalar(T.gg[P, 0:1], d, -STEP, DOWN, A.is_ge, A.mult).then_inc(sem.c2, 1)
+    ve.wait_ge(sem.c2, 2)
+    ve.tensor_scalar(T.aa[P, 1:2], d, 0.0, T.gg[P, 1:2], A.is_le, A.max).then_inc(sem.c4, 1)
+    ve.tensor_scalar(T.aa[P, 0:1], d, 0.0, T.gg[P, 0:1], A.is_ge, A.max).then_inc(sem.c3, 1)
+    se.wait_ge(sem.c4, 1)
+    se.activation(T.o0[P, 0:129], T.pb[P, 0:129], F.Copy, scale=T.aa[P, 1:2]).then_inc(sem.c5, 1)
+    ve.wait_ge(sem.c3, 1)
+    ve.tensor_scalar(T.tt[P, :], T.pa[P, 0:129], T.aa[P, 0:1], None, A.mult).then_inc(sem.c6, 1)
+    ve.wait_ge(sem.c6, 1)
+    ve.wait_ge(sem.c5, 1)
+    ve.tensor_tensor(T.zz[P, :], T.tt[P, :], T.o0[P, 0:129], A.add).then_inc(sem.c7, 1)
+    ve.wait_ge(sem.c7, 1)
+    ve.reciprocal(T.rr[P, :], T.zz[P, 128:129]).then_inc(sem.c8, 1)
+    ve.wait_ge(sem.c8, 1)
+    ve.tensor_scalar(T.yb[P, :], T.zz[P, 0:128], T.rr[P, :], None, A.mult).then_inc(sem.c9, 1)
+    sy.wait_ge(sem.c9, 1)
+    sy.dma_start(T.y[:], T.yb[P, :]).then_inc(sem.st, 16)
+    sy.wait_ge(sem.st, 16)
+
+
+def rank_program(g, core, T, topo):
+    job, home, feeds = _plan(T, topo)
+    if core in job:
+        _worker(g, core, T, topo, job)
+    elif T.rank_of(core) is not None:
+        _rank(g, core, T, topo, job, home, feeds)

@@ -8,7 +8,7 @@ NR = 8
 NKV = 16
 
 STEP = 64.0
-MAGIC = 12582912.0
+MAGIC = 805306368.0
 DOWN = math.exp(-STEP)
 
 SCRATCH = {
@@ -19,7 +19,7 @@ SCRATCH = {
     "vb": ("sbuf", [128, 256], "bfloat16"),
     "mask": ("sbuf", [128, 128], "float32"),
     "ident": ("sbuf", [128, 128], "bfloat16"),
-    "mx": ("sbuf", [128, 4], "float32"),
+    "mx": ("sbuf", [128, 2], "float32"),
     "ls": ("sbuf", [128, 4], "float32"),
     "p0": ("sbuf", [128, 256], "bfloat16"),
     "p1": ("sbuf", [128, 256], "bfloat16"),
@@ -29,9 +29,8 @@ SCRATCH = {
     "res1": ("sbuf", [128, 130], "bfloat16"),
     "pa": ("sbuf", [128, 130], "bfloat16"),
     "pb": ("sbuf", [128, 130], "bfloat16"),
-    "dd": ("sbuf", [128, 1], "float32"),
-    "gg": ("sbuf", [128, 2], "float32"),
-    "aa": ("sbuf", [128, 2], "float32"),
+    "th": ("sbuf", [128, 3], "float32"),
+    "cc": ("sbuf", [128, 4], "float32"),
     "tt": ("sbuf", [128, 129], "float32"),
     "zz": ("sbuf", [128, 129], "float32"),
     "rr": ("sbuf", [128, 1], "float32"),
@@ -46,9 +45,9 @@ SCRATCH = {
     "tp11": ("psum", [128, 1024], "bfloat16"),
 }
 
-_BATCH_SEMS = ["sS", "sA", "sB", "sM", "sPa", "sPb", "sTa", "sTb", "sCa", "sCb", "sO", "sL", "sR"]
-SEMAPHORES = (["ql", "kl", "vl", "snt", "qa", "qf", "ka", "va", "res", "i0", "i1", "i2", "st",
-               "c1", "c2", "c3", "c4", "c5", "c6", "c7", "c8", "c9"]
+_BATCH_SEMS = ["sS", "sA", "sM", "sPa", "sPb", "sTa", "sTb", "sCa", "sCb", "sO", "sL", "sR"]
+SEMAPHORES = (["ql", "kl", "vl", "snt", "qa", "qf", "ka", "va", "resa", "resb", "i0", "i1", "i2", "st",
+               "c1", "c2", "c5", "c7", "c8", "c9"]
               + [n + str(b) for b in (0, 1) for n in _BATCH_SEMS])
 
 
@@ -123,7 +122,7 @@ def _worker(g, core, T, topo, job):
         S = lambda n: sem[n + str(b)]
         q, s, o, p, pt, res = (T.qown, T.qfar)[b], T["s%d" % b], T["o%d" % b], T["p%d" % b], T["pt%d" % b], T["res%d" % b]
         tp = [T["tp%d0" % b], T["tp%d1" % b]]
-        mx, kq = T.mx[:, 2 * b:2 * b + 1], T.mx[:, 2 * b + 1:2 * b + 2]
+        mx = T.mx[:, b:b + 1]
         nm = res[:, 129:130]
         if b == 0:
             te.wait_ge(sem.qa, q_all)
@@ -132,11 +131,9 @@ def _worker(g, core, T, topo, job):
             te.wait_ge(sem.qf, nf)
         te.matmul(s[:, 0:256], q[:], T.kb[:], True, True).then_inc(S("sS"), 1)
         ve.wait_ge(S("sS"), 1)
-        ve.tensor_reduce(mx, s[:, 0:256], AxisListType.X, A.max).then_inc(S("sA"), 1)
+        ve.tensor_reduce(mx, s[:, 0:256], AxisListType.X, A.max, negate=True).then_inc(S("sA"), 1)
         ve.wait_ge(S("sA"), 1)
-        ve.tensor_scalar(kq, mx, 1.0 / STEP, MAGIC, A.mult, A.add).then_inc(S("sB"), 1)
-        ve.wait_ge(S("sB"), 1)
-        ve.tensor_scalar(nm, kq, MAGIC, -STEP, A.subtract, A.mult).then_inc(S("sM"), 1)
+        ve.tensor_scalar(nm, mx, MAGIC, MAGIC, A.add, A.subtract).then_inc(S("sM"), 1)
         se.wait_ge(S("sM"), 1)
         for j, n in enumerate(("sPa", "sPb")):
             se.activation(p[:, 128 * j:128 * j + 128], s[:, 128 * j:128 * j + 128], F.Exp, bias=nm,
@@ -163,13 +160,13 @@ def _worker(g, core, T, topo, job):
         g.wait_ge(S("sM"), 1)
         g.wait_ge(S("sL"), 1)
         g.wait_ge(S("sR"), 1)
-        sent += _fan(g, T, topo, core, (own, far)[b], res[:], (T.pa, T.pb)[b][:], sem.res, NR)
+        sent += _fan(g, T, topo, core, (own, far)[b], res[:], (T.pa, T.pb)[b][:], (sem.resa, sem.resb)[b], NR)
     g.wait_ge(sem.snt, sent)
 
 
 def _rank(g, core, T, topo, job, home, feeds):
     sem = T.sem
-    A, F = AluOpType, ActivationFunctionType
+    A = AluOpType
     ve, se, sy = g.vector, g.scalar, g.sync
     w, h = home[core]
     partner = job[w][0]
@@ -190,24 +187,25 @@ def _rank(g, core, T, topo, job, home, feeds):
         sent += _fan(g, T, topo, core, feeds[core], T.vb[:], T.vb[:], sem.va, NKV)
     g.wait_ge(sem.snt, sent)
 
-    both = _engines(topo, w, job[w][1], NR)[1] + _engines(topo, partner, job[partner][2], NR)[1]
+    n_a = _engines(topo, w, job[w][1], NR)[1]
+    n_b = _engines(topo, partner, job[partner][2], NR)[1]
     P = slice(64 * h, 64 * h + 64)
-    d = T.dd[P, :]
-    ve.wait_ge(sem.res, both)
-    se.wait_ge(sem.res, both)
-    ve.tensor_tensor(d, T.pb[P, 129:130], T.pa[P, 129:130], A.subtract).then_inc(sem.c1, 1)
-    ve.wait_ge(sem.c1, 1)
-    ve.tensor_scalar(T.gg[P, 1:2], d, STEP, DOWN, A.is_le, A.mult).then_inc(sem.c2, 1)
-    ve.tensor_scalar(T.gg[P, 0:1], d, -STEP, DOWN, A.is_ge, A.mult).then_inc(sem.c2, 1)
-    ve.wait_ge(sem.c2, 2)
-    ve.tensor_scalar(T.aa[P, 1:2], d, 0.0, T.gg[P, 1:2], A.is_le, A.max).then_inc(sem.c4, 1)
-    ve.tensor_scalar(T.aa[P, 0:1], d, 0.0, T.gg[P, 0:1], A.is_ge, A.max).then_inc(sem.c3, 1)
-    se.wait_ge(sem.c4, 1)
-    se.activation(T.o0[P, 0:129], T.pb[P, 0:129], F.Copy, scale=T.aa[P, 1:2]).then_inc(sem.c5, 1)
-    ve.wait_ge(sem.c3, 1)
-    ve.tensor_scalar(T.tt[P, :], T.pa[P, 0:129], T.aa[P, 0:1], None, A.mult).then_inc(sem.c6, 1)
-    ve.wait_ge(sem.c6, 1)
-    ve.wait_ge(sem.c5, 1)
+    na, nb = T.pa[P, 129:130], T.pb[P, 129:130]
+    up, dn, at = T.th[P, 0:1], T.th[P, 1:2], T.th[P, 2:3]
+    ve.wait_ge(sem.resa, n_a)
+    ve.tensor_scalar(up, na, STEP, None, A.add).then_inc(sem.c1, 1)
+    ve.tensor_scalar(dn, na, -STEP, None, A.add).then_inc(sem.c1, 1)
+    ve.tensor_copy(at, na).then_inc(sem.c1, 1)
+    ve.wait_ge(sem.c1, 3)
+    ve.wait_ge(sem.resb, n_b)
+    ve.tensor_scalar(T.cc[P, 2:3], nb, up, None, A.is_le).then_inc(sem.c2, 1)
+    ve.tensor_scalar(T.cc[P, 3:4], nb, at, DOWN, A.is_le, A.max).then_inc(sem.c2, 1)
+    ve.tensor_scalar(T.cc[P, 0:1], nb, dn, None, A.is_ge).then_inc(sem.c2, 1)
+    ve.tensor_scalar(T.cc[P, 1:2], nb, at, DOWN, A.is_ge, A.max).then_inc(sem.c2, 1)
+    ve.wait_ge(sem.c2, 4)
+    ve.tensor_scalar(T.o0[P, 0:129], T.pb[P, 0:129], T.cc[P, 2:3], T.cc[P, 3:4], A.mult, A.mult).then_inc(sem.c5, 1)
+    ve.tensor_scalar(T.tt[P, :], T.pa[P, 0:129], T.cc[P, 0:1], T.cc[P, 1:2], A.mult, A.mult).then_inc(sem.c5, 1)
+    ve.wait_ge(sem.c5, 2)
     ve.tensor_tensor(T.zz[P, :], T.tt[P, :], T.o0[P, 0:129], A.add).then_inc(sem.c7, 1)
     ve.wait_ge(sem.c7, 1)
     ve.reciprocal(T.rr[P, :], T.zz[P, 128:129]).then_inc(sem.c8, 1)

@@ -7,47 +7,49 @@ NF = 8
 NR = 8
 NKV = 16
 
-STEP = 64.0
-MAGIC = 805306368.0
-DOWN = math.exp(-STEP)
+LOW = -1.0e29
+OFF = 1.0e9
+VW = 136
+RW = 131
 
 SCRATCH = {
     "qs": ("sbuf", [128, 64], "bfloat16"),
     "qown": ("sbuf", [128, 128], "bfloat16"),
     "qfar": ("sbuf", [128, 128], "bfloat16"),
     "kb": ("sbuf", [128, 256], "bfloat16"),
-    "vb": ("sbuf", [128, 256], "bfloat16"),
+    "va": ("sbuf", [128, 2 * VW], "bfloat16"),
     "mask": ("sbuf", [128, 128], "float32"),
     "ident": ("sbuf", [128, 128], "bfloat16"),
-    "mx": ("sbuf", [128, 2], "float32"),
-    "ls": ("sbuf", [128, 4], "float32"),
+    "nid": ("sbuf", [128, 128], "bfloat16"),
+    "low": ("sbuf", [128, 384], "bfloat16"),
+    "mb0": ("sbuf", [128, 384], "bfloat16"),
+    "mb1": ("sbuf", [128, 384], "bfloat16"),
     "p0": ("sbuf", [128, 256], "bfloat16"),
     "p1": ("sbuf", [128, 256], "bfloat16"),
-    "pt0": ("sbuf", [128, 256], "bfloat16"),
-    "pt1": ("sbuf", [128, 256], "bfloat16"),
-    "res0": ("sbuf", [128, 130], "bfloat16"),
-    "res1": ("sbuf", [128, 130], "bfloat16"),
-    "pa": ("sbuf", [128, 130], "bfloat16"),
-    "pb": ("sbuf", [128, 130], "bfloat16"),
-    "th": ("sbuf", [128, 3], "float32"),
-    "cc": ("sbuf", [128, 4], "float32"),
-    "tt": ("sbuf", [128, 129], "float32"),
-    "zz": ("sbuf", [128, 129], "float32"),
+    "res0": ("sbuf", [128, RW], "bfloat16"),
+    "res1": ("sbuf", [128, RW], "bfloat16"),
+    "pa": ("sbuf", [128, RW], "bfloat16"),
+    "pb": ("sbuf", [128, RW], "bfloat16"),
+    "off": ("sbuf", [128, 64], "float32"),
+    "ma": ("sbuf", [128, 64], "float32"),
+    "mn": ("sbuf", [128, 64], "float32"),
+    "da": ("sbuf", [128, 64], "bfloat16"),
+    "db": ("sbuf", [128, 64], "bfloat16"),
     "rr": ("sbuf", [128, 1], "float32"),
     "yb": ("sbuf", [128, 128], "bfloat16"),
     "s0": ("psum", [128, 512], "float32"),
     "s1": ("psum", [128, 512], "float32"),
+    "ta0": ("psum", [128, 512], "float32"),
+    "tb0": ("psum", [128, 512], "float32"),
+    "ta1": ("psum", [128, 512], "float32"),
+    "tb1": ("psum", [128, 512], "float32"),
     "o0": ("psum", [128, 512], "float32"),
     "o1": ("psum", [128, 512], "float32"),
-    "tp00": ("psum", [128, 1024], "bfloat16"),
-    "tp01": ("psum", [128, 1024], "bfloat16"),
-    "tp10": ("psum", [128, 1024], "bfloat16"),
-    "tp11": ("psum", [128, 1024], "bfloat16"),
 }
 
-_BATCH_SEMS = ["sS", "sA", "sM", "sPa", "sPb", "sTa", "sTb", "sCa", "sCb", "sO", "sL", "sR"]
-SEMAPHORES = (["ql", "kl", "vl", "snt", "qa", "qf", "ka", "va", "resa", "resb", "i0", "i1", "i2", "st",
-               "c1", "c2", "c5", "c7", "c8", "c9"]
+_BATCH_SEMS = ["sS", "sM", "sTa", "sTb", "sPa", "sPb", "sO", "sL", "sR"]
+SEMAPHORES = (["ql", "kl", "vl", "on", "snt", "qa", "qf", "ka", "va", "resa", "resb", "i0", "i1", "i2", "i3", "i4",
+               "i5", "st", "c1", "c2", "c3", "c5", "c8", "c9"]
               + [n + str(b) for b in (0, 1) for n in _BATCH_SEMS])
 
 
@@ -105,10 +107,17 @@ def _worker(g, core, T, topo, job):
     te, ve, se = g.tensor, g.vector, g.scalar
 
     ve.memset(T.mask[:], 0.0).then_inc(sem.i0, 1)
+    ve.memset(T.low[:], LOW).then_inc(sem.i5, 1)
+    ve.memset(T.s0[:, 256:384], LOW).then_inc(sem.i4, 1)
+    ve.memset(T.s1[:, 256:384], LOW).then_inc(sem.i4, 1)
     g.wait_ge(sem.i0, 1)
     g.affine_select(T.mask[:], T.mask[:], [[-1, 128]], A.is_equal, -200.0, 0, 1).then_inc(sem.i1, 1)
     se.wait_ge(sem.i1, 1)
     se.activation(T.ident[:], T.mask[:], F.Exp).then_inc(sem.i2, 1)
+    ve.wait_ge(sem.i2, 1)
+    ve.tensor_scalar(T.nid[:], T.ident[:], -1.0, None, A.mult).then_inc(sem.i3, 1)
+    ve.wait_ge(sem.i5, 1)
+    ve.wait_ge(sem.i4, 2)
 
     q_all = sum(_q_engines(topo, c, core)[1] for c in own)
     g.wait_ge(sem.qa, q_all)
@@ -116,65 +125,94 @@ def _worker(g, core, T, topo, job):
     rid, pid, _ = topo.addr(partner)
     g.remote_dma(out_ap=T.qfar[:], in_ap=T.qown[:], remote_sem=sem.qf, local_sem=sem.snt, pid=pid, routing_id=rid,
                  dma_engine_mask=m)
-    sent = nf
+    sent = [nf]
 
-    for b in (0, 1):
-        S = lambda n: sem[n + str(b)]
-        q, s, o, p, pt, res = (T.qown, T.qfar)[b], T["s%d" % b], T["o%d" % b], T["p%d" % b], T["pt%d" % b], T["res%d" % b]
-        tp = [T["tp%d0" % b], T["tp%d1" % b]]
-        mx = T.mx[:, b:b + 1]
-        nm = res[:, 129:130]
+    def S(n, b):
+        return sem[n + str(b)]
+
+    def scores(b):
+        q, s = (T.qown, T.qfar)[b], T["s%d" % b]
         if b == 0:
             te.wait_ge(sem.qa, q_all)
             te.wait_ge(sem.ka, NKV)
+            te.wait_ge(sem.i4, 2)
         else:
             te.wait_ge(sem.qf, nf)
-        te.matmul(s[:, 0:256], q[:], T.kb[:], True, True).then_inc(S("sS"), 1)
-        ve.wait_ge(S("sS"), 1)
-        ve.tensor_reduce(mx, s[:, 0:256], AxisListType.X, A.max, negate=True).then_inc(S("sA"), 1)
-        ve.wait_ge(S("sA"), 1)
-        ve.tensor_scalar(nm, mx, MAGIC, MAGIC, A.add, A.subtract).then_inc(S("sM"), 1)
-        se.wait_ge(S("sM"), 1)
-        for j, n in enumerate(("sPa", "sPb")):
-            se.activation(p[:, 128 * j:128 * j + 128], s[:, 128 * j:128 * j + 128], F.Exp, bias=nm,
-                          accum_out=T.ls[:, 2 * b + j:2 * b + j + 1]).then_inc(S(n), 1)
+        te.matmul(s[:, 0:256], q[:], T.kb[:], True, True).then_inc(S("sS", b), 1)
+        te.matmul(T["ta%d" % b][:, 0:128], T.kb[:, 0:128], q[:], True, False)
+        te.matmul(T["tb%d" % b][:, 0:128], T.kb[:, 128:256], q[:], True, False)
+
+    def shift(b):
+        s, mb, res = T["s%d" % b], T["mb%d" % b], T["res%d" % b]
+        ve.wait_ge(S("sS", b), 1)
+        ve.tensor_tensor_scan(mb[:], s[:, 0:384], T.low[:], LOW, A.max, A.max).then_inc(S("sM", b), 1)
+        ve.wait_ge(S("sM", b), 1)
+        ve.tensor_copy(res[:, 129:130], mb[:, 383:384]).then_inc(S("sL", b), 1)
+        ve.tensor_scalar(res[:, 130:131], mb[:, 383:384], -1.0, None, A.mult).then_inc(S("sL", b), 1)
+
+    def shifted(b):
+        mb = T["mb%d" % b]
         if b == 0:
-            te.wait_ge(sem.i2, 1)
-        for j, (n, n2) in enumerate((("sPa", "sTa"), ("sPb", "sTb"))):
-            te.wait_ge(S(n), 1)
-            te.transpose(tp[j][:, 0:128], p[:, 128 * j:128 * j + 128], T.ident[:]).then_inc(S(n2), 1)
-        for j, (n, n2) in enumerate((("sTa", "sCa"), ("sTb", "sCb"))):
-            ve.wait_ge(S(n), 1)
-            ve.tensor_copy(pt[:, 128 * j:128 * j + 128], tp[j][:, 0:128]).then_inc(S(n2), 1)
+            te.wait_ge(sem.i3, 1)
+        te.wait_ge(S("sM", b), 1)
+        te.matmul(T["ta%d" % b][:, 0:128], mb[:, 256:384], T.nid[:], False, True).then_inc(S("sTa", b), 1)
+        te.matmul(T["tb%d" % b][:, 0:128], mb[:, 256:384], T.nid[:], False, True).then_inc(S("sTb", b), 1)
+
+    def weights(b):
+        p = T["p%d" % b]
+        se.wait_ge(S("sTa", b), 1)
+        se.activation(p[:, 0:128], T["ta%d" % b][:, 0:128], F.Exp).then_inc(S("sPa", b), 1)
+        se.wait_ge(S("sTb", b), 1)
+        se.activation(p[:, 128:256], T["tb%d" % b][:, 0:128], F.Exp).then_inc(S("sPb", b), 1)
+
+    def values(b):
+        p, o = T["p%d" % b], T["o%d" % b]
         if b == 0:
             te.wait_ge(sem.va, NKV)
-        te.wait_ge(S("sCa"), 1)
-        te.matmul(o[:, 0:128], pt[:, 0:128], T.vb[:, 0:128], True, False)
-        te.wait_ge(S("sCb"), 1)
-        te.matmul(o[:, 0:128], pt[:, 128:256], T.vb[:, 128:256], False, True).then_inc(S("sO"), 1)
-        ve.wait_ge(S("sPa"), 1)
-        ve.wait_ge(S("sPb"), 1)
-        ve.tensor_tensor(res[:, 128:129], T.ls[:, 2 * b:2 * b + 1], T.ls[:, 2 * b + 1:2 * b + 2], A.add).then_inc(S("sL"), 1)
-        ve.wait_ge(S("sO"), 1)
-        ve.tensor_copy(res[:, 0:128], o[:, 0:128]).then_inc(S("sR"), 1)
-        g.wait_ge(S("sM"), 1)
-        g.wait_ge(S("sL"), 1)
-        g.wait_ge(S("sR"), 1)
-        sent += _fan(g, T, topo, core, (own, far)[b], res[:], (T.pa, T.pb)[b][:], (sem.resa, sem.resb)[b], NR)
-    g.wait_ge(sem.snt, sent)
+        te.wait_ge(S("sPa", b), 1)
+        te.matmul(o[:, 0:129], p[:, 0:128], T.va[:, 0:129], True, False)
+        te.wait_ge(S("sPb", b), 1)
+        te.matmul(o[:, 0:129], p[:, 128:256], T.va[:, VW:VW + 129], False, True).then_inc(S("sO", b), 1)
+
+    def result(b):
+        res = T["res%d" % b]
+        ve.wait_ge(S("sO", b), 1)
+        ve.tensor_copy(res[:, 0:129], T["o%d" % b][:, 0:129]).then_inc(S("sR", b), 1)
+        g.wait_ge(S("sL", b), 2)
+        g.wait_ge(S("sR", b), 1)
+        sent[0] += _fan(g, T, topo, core, (own, far)[b], res[:], (T.pa, T.pb)[b][:], (sem.resa, sem.resb)[b], NR)
+
+    scores(0)
+    shift(0)
+    shifted(0)
+    weights(0)
+    scores(1)
+    shift(1)
+    values(0)
+    result(0)
+    shifted(1)
+    weights(1)
+    values(1)
+    result(1)
+    g.wait_ge(sem.snt, sent[0])
 
 
 def _rank(g, core, T, topo, job, home, feeds):
     sem = T.sem
-    A = AluOpType
-    ve, se, sy = g.vector, g.scalar, g.sync
+    A, F = AluOpType, ActivationFunctionType
+    te, ve, se, sy = g.tensor, g.vector, g.scalar, g.sync
     w, h = home[core]
     partner = job[w][0]
+    P = slice(64 * h, 64 * h + 64)
 
     sy.dma_start(T.qs[:], T.q[:]).then_inc(sem.ql, 16)
     if core in feeds:
         se.dma_start(T.kb[:], T.k[:]).then_inc(sem.kl, 16)
-        sy.dma_start(T.vb[:], T.v[:]).then_inc(sem.vl, 16)
+        sy.dma_start(T.va[:, 0:128], T.v[:, 0:128]).then_inc(sem.vl, 16)
+        se.dma_start(T.va[:, VW:VW + 128], T.v[:, 128:256]).then_inc(sem.vl, 16)
+        ve.memset(T.va[:, 128:VW], 1.0).then_inc(sem.on, 1)
+        ve.memset(T.va[:, VW + 128:2 * VW], 1.0).then_inc(sem.on, 1)
+    ve.memset(T.mask[P, 0:64], 200.0).then_inc(sem.i0, 1)
     g.wait_ge(sem.ql, 16)
     m, sent = _q_engines(topo, core, w)
     rid, pid, _ = topo.addr(w)
@@ -183,36 +221,39 @@ def _rank(g, core, T, topo, job, home, feeds):
     if core in feeds:
         g.wait_ge(sem.kl, 16)
         sent += _fan(g, T, topo, core, feeds[core], T.kb[:], T.kb[:], sem.ka, NKV)
-        g.wait_ge(sem.vl, 16)
-        sent += _fan(g, T, topo, core, feeds[core], T.vb[:], T.vb[:], sem.va, NKV)
+        g.wait_ge(sem.vl, 32)
+        g.wait_ge(sem.on, 2)
+        sent += _fan(g, T, topo, core, feeds[core], T.va[:], T.va[:], sem.va, NKV)
+    g.wait_ge(sem.i0, 1)
+    g.affine_select(T.mask[P, 0:64], T.mask[P, 0:64], [[-1, 64]], A.is_equal, -200.0, 0, 1).then_inc(sem.i1, 1)
+    se.wait_ge(sem.i1, 1)
+    se.activation(T.ident[P, 0:64], T.mask[P, 0:64], F.Sigmoid).then_inc(sem.i2, 1)
+    ve.wait_ge(sem.i2, 1)
+    ve.tensor_scalar(T.off[P, :], T.ident[P, 0:64], 1.0, OFF, A.subtract, A.mult).then_inc(sem.i3, 1)
     g.wait_ge(sem.snt, sent)
 
     n_a = _engines(topo, w, job[w][1], NR)[1]
     n_b = _engines(topo, partner, job[partner][2], NR)[1]
-    P = slice(64 * h, 64 * h + 64)
-    na, nb = T.pa[P, 129:130], T.pb[P, 129:130]
-    up, dn, at = T.th[P, 0:1], T.th[P, 1:2], T.th[P, 2:3]
+    ve.wait_ge(sem.i3, 1)
     ve.wait_ge(sem.resa, n_a)
-    ve.tensor_scalar(up, na, STEP, None, A.add).then_inc(sem.c1, 1)
-    ve.tensor_scalar(dn, na, -STEP, None, A.add).then_inc(sem.c1, 1)
-    ve.tensor_copy(at, na).then_inc(sem.c1, 1)
-    ve.wait_ge(sem.c1, 3)
-    ve.wait_ge(sem.resb, n_b)
-    ve.tensor_scalar(T.cc[P, 2:3], nb, up, None, A.is_le).then_inc(sem.c2, 1)
-    ve.tensor_scalar(T.cc[P, 3:4], nb, at, DOWN, A.is_le, A.max).then_inc(sem.c2, 1)
-    ve.tensor_scalar(T.cc[P, 0:1], nb, dn, None, A.is_ge).then_inc(sem.c2, 1)
-    ve.tensor_scalar(T.cc[P, 1:2], nb, at, DOWN, A.is_ge, A.max).then_inc(sem.c2, 1)
-    ve.wait_ge(sem.c2, 4)
-    ve.tensor_scalar(T.o0[P, 0:129], T.pb[P, 0:129], T.cc[P, 2:3], T.cc[P, 3:4], A.mult, A.mult).then_inc(sem.c5, 1)
-    ve.tensor_scalar(T.tt[P, :], T.pa[P, 0:129], T.cc[P, 0:1], T.cc[P, 1:2], A.mult, A.mult).then_inc(sem.c5, 1)
-    ve.wait_ge(sem.c5, 2)
-    ve.tensor_tensor(T.zz[P, :], T.tt[P, :], T.o0[P, 0:129], A.add).then_inc(sem.c7, 1)
-    ve.wait_ge(sem.c7, 1)
-    ve.reciprocal(T.rr[P, :], T.zz[P, 128:129]).then_inc(sem.c8, 1)
+    ve.tensor_scalar(T.mn[P, :], T.off[P, :], T.pa[P, 130:131], None, A.add).then_inc(sem.c1, 1)
+    ve.tensor_scalar(T.ma[P, :], T.off[P, :], T.pa[P, 129:130], None, A.add).then_inc(sem.c1, 1)
+    se.wait_ge(sem.c1, 2)
+    se.wait_ge(sem.resb, n_b)
+    se.activation(T.db[P, :], T.mn[P, :], F.Sigmoid, bias=T.pb[P, 129:130]).then_inc(sem.c2, 1)
+    se.activation(T.da[P, :], T.ma[P, :], F.Sigmoid, bias=T.pb[P, 130:131]).then_inc(sem.c3, 1)
+    te.wait_ge(sem.resa, n_a)
+    te.wait_ge(sem.resb, n_b)
+    te.wait_ge(sem.c2, 1)
+    te.matmul(T.o0[0:64, 0:129], T.db[P, :], T.pb[P, 0:129], True, False)
+    te.wait_ge(sem.c3, 1)
+    te.matmul(T.o0[0:64, 0:129], T.da[P, :], T.pa[P, 0:129], False, True).then_inc(sem.c5, 1)
+    ve.wait_ge(sem.c5, 1)
+    ve.reciprocal(T.rr[0:64, :], T.o0[0:64, 128:129]).then_inc(sem.c8, 1)
     ve.wait_ge(sem.c8, 1)
-    ve.tensor_scalar(T.yb[P, :], T.zz[P, 0:128], T.rr[P, :], None, A.mult).then_inc(sem.c9, 1)
+    ve.tensor_scalar(T.yb[0:64, :], T.o0[0:64, 0:128], T.rr[0:64, :], None, A.mult).then_inc(sem.c9, 1)
     sy.wait_ge(sem.c9, 1)
-    sy.dma_start(T.y[:], T.yb[P, :]).then_inc(sem.st, 16)
+    sy.dma_start(T.y[:], T.yb[0:64, :]).then_inc(sem.st, 16)
     sy.wait_ge(sem.st, 16)
 
 

@@ -10,10 +10,11 @@ NKV = 16
 LOW = -1.0e29
 OFF = 1.0e9
 VW = 136
-RW = 131
+RW = 129
 
 SCRATCH = {
     "qs": ("sbuf", [128, 64], "bfloat16"),
+    "qx": ("sbuf", [128, 64], "bfloat16"),
     "qown": ("sbuf", [128, 128], "bfloat16"),
     "qfar": ("sbuf", [128, 128], "bfloat16"),
     "kb": ("sbuf", [128, 256], "bfloat16"),
@@ -26,8 +27,12 @@ SCRATCH = {
     "mb1": ("sbuf", [128, 384], "bfloat16"),
     "p0": ("sbuf", [128, 256], "bfloat16"),
     "p1": ("sbuf", [128, 256], "bfloat16"),
+    "sh0": ("sbuf", [128, 2], "bfloat16"),
+    "sh1": ("sbuf", [128, 2], "bfloat16"),
     "res0": ("sbuf", [128, RW], "bfloat16"),
     "res1": ("sbuf", [128, RW], "bfloat16"),
+    "sa": ("sbuf", [128, 2], "bfloat16"),
+    "sb": ("sbuf", [128, 2], "bfloat16"),
     "pa": ("sbuf", [128, RW], "bfloat16"),
     "pb": ("sbuf", [128, RW], "bfloat16"),
     "off": ("sbuf", [128, 64], "float32"),
@@ -48,8 +53,8 @@ SCRATCH = {
 }
 
 _BATCH_SEMS = ["sS", "sM", "sTa", "sTb", "sPa", "sPb", "sO", "sL", "sR"]
-SEMAPHORES = (["ql", "kl", "vl", "on", "snt", "qa", "qf", "ka", "va", "resa", "resb", "i0", "i1", "i2", "i3", "i4",
-               "i5", "st", "c1", "c2", "c3", "c5", "c8", "c9"]
+SEMAPHORES = (["ql", "kl", "vl", "on", "snt", "qa", "qf", "qr", "ka", "va", "sha", "shb", "resa", "resb", "i0", "i1",
+               "i2", "i3", "i4", "i5", "st", "c1", "c2", "c3", "c5", "c8", "c9"]
               + [n + str(b) for b in (0, 1) for n in _BATCH_SEMS])
 
 
@@ -63,6 +68,12 @@ def _engines(topo, src, dsts, n):
     for e in bits[::len(bits) // n][:n]:
         m |= 1 << e
     return m, n
+
+
+def _halves(topo, src, dsts):
+    m, n = _engines(topo, src, dsts, 2 * NQ)
+    bits = [e for e in range(16) if (m >> e) & 1]
+    return sum(1 << e for e in bits[0::2]), sum(1 << e for e in bits[1::2]), n // 2
 
 
 def _plan(T, topo):
@@ -88,8 +99,17 @@ def _plan(T, topo):
     return job, home, feeds
 
 
-def _q_engines(topo, c, w):
-    return _engines(topo, c, [w], NKV if topo.chip(c) == topo.chip(w) else NQ)
+def _q_counts(topo, pair, w, partner):
+    at_w = at_p = 0
+    for i, c in enumerate(pair):
+        if topo.may_write(c, partner):
+            n = _halves(topo, c, [w, partner])[2]
+            at_w += n
+            at_p += n
+        else:
+            at_w += _engines(topo, c, [pair[1 - i], w], NQ)[1]
+            at_p += _engines(topo, pair[1 - i], [partner], NF)[1]
+    return at_w, at_p
 
 
 def _fan(g, T, topo, core, dsts, src, dst, sem, n):
@@ -119,13 +139,9 @@ def _worker(g, core, T, topo, job):
     ve.wait_ge(sem.i5, 1)
     ve.wait_ge(sem.i4, 2)
 
-    q_all = sum(_q_engines(topo, c, core)[1] for c in own)
-    g.wait_ge(sem.qa, q_all)
-    m, nf = _engines(topo, core, [partner], NF)
-    rid, pid, _ = topo.addr(partner)
-    g.remote_dma(out_ap=T.qfar[:], in_ap=T.qown[:], remote_sem=sem.qf, local_sem=sem.snt, pid=pid, routing_id=rid,
-                 dma_engine_mask=m)
-    sent = [nf]
+    q_own = _q_counts(topo, own, core, partner)[0]
+    q_far = _q_counts(topo, far, partner, core)[1]
+    sent = [0]
 
     def S(n, b):
         return sem[n + str(b)]
@@ -133,22 +149,24 @@ def _worker(g, core, T, topo, job):
     def scores(b):
         q, s = (T.qown, T.qfar)[b], T["s%d" % b]
         if b == 0:
-            te.wait_ge(sem.qa, q_all)
+            te.wait_ge(sem.qa, q_own)
             te.wait_ge(sem.ka, NKV)
             te.wait_ge(sem.i4, 2)
         else:
-            te.wait_ge(sem.qf, nf)
+            te.wait_ge(sem.qf, q_far)
         te.matmul(s[:, 0:256], q[:], T.kb[:], True, True).then_inc(S("sS", b), 1)
         te.matmul(T["ta%d" % b][:, 0:128], T.kb[:, 0:128], q[:], True, False)
         te.matmul(T["tb%d" % b][:, 0:128], T.kb[:, 128:256], q[:], True, False)
 
     def shift(b):
-        s, mb, res = T["s%d" % b], T["mb%d" % b], T["res%d" % b]
+        s, mb, sh = T["s%d" % b], T["mb%d" % b], T["sh%d" % b]
         ve.wait_ge(S("sS", b), 1)
         ve.tensor_tensor_scan(mb[:], s[:, 0:384], T.low[:], LOW, A.max, A.max).then_inc(S("sM", b), 1)
         ve.wait_ge(S("sM", b), 1)
-        ve.tensor_copy(res[:, 129:130], mb[:, 383:384]).then_inc(S("sL", b), 1)
-        ve.tensor_scalar(res[:, 130:131], mb[:, 383:384], -1.0, None, A.mult).then_inc(S("sL", b), 1)
+        ve.tensor_copy(sh[:, 0:1], mb[:, 383:384]).then_inc(S("sL", b), 1)
+        ve.tensor_scalar(sh[:, 1:2], mb[:, 383:384], -1.0, None, A.mult).then_inc(S("sL", b), 1)
+        g.wait_ge(S("sL", b), 2)
+        sent[0] += _fan(g, T, topo, core, (own, far)[b], sh[:], (T.sa, T.sb)[b][:], (sem.sha, sem.shb)[b], NR)
 
     def shifted(b):
         mb = T["mb%d" % b]
@@ -177,23 +195,13 @@ def _worker(g, core, T, topo, job):
     def result(b):
         res = T["res%d" % b]
         ve.wait_ge(S("sO", b), 1)
-        ve.tensor_copy(res[:, 0:129], T["o%d" % b][:, 0:129]).then_inc(S("sR", b), 1)
-        g.wait_ge(S("sL", b), 2)
+        ve.tensor_copy(res[:], T["o%d" % b][:, 0:129]).then_inc(S("sR", b), 1)
         g.wait_ge(S("sR", b), 1)
         sent[0] += _fan(g, T, topo, core, (own, far)[b], res[:], (T.pa, T.pb)[b][:], (sem.resa, sem.resb)[b], NR)
 
-    scores(0)
-    shift(0)
-    shifted(0)
-    weights(0)
-    scores(1)
-    shift(1)
-    values(0)
-    result(0)
-    shifted(1)
-    weights(1)
-    values(1)
-    result(1)
+    for stage in (scores, shift, shifted, weights, values, result):
+        stage(0)
+        stage(1)
     g.wait_ge(sem.snt, sent[0])
 
 
@@ -202,8 +210,20 @@ def _rank(g, core, T, topo, job, home, feeds):
     A, F = AluOpType, ActivationFunctionType
     te, ve, se, sy = g.tensor, g.vector, g.scalar, g.sync
     w, h = home[core]
-    partner = job[w][0]
+    partner, pair = job[w][0], job[w][1]
+    other = pair[1 - h]
     P = slice(64 * h, 64 * h + 64)
+    C = slice(64 * h, 64 * h + 64)
+    CO = slice(64 * (1 - h), 64 * (1 - h) + 64)
+
+    def mask_call():
+        g.wait_ge(sem.i0, 1)
+        g.affine_select(T.mask[P, 0:64], T.mask[P, 0:64], [[-1, 64]], A.is_equal, -200.0, 0, 1).then_inc(sem.i1, 1)
+
+    def send(dst_core, out_ap, in_ap, rsem, m):
+        rid, pid, _ = topo.addr(dst_core)
+        g.remote_dma(out_ap=out_ap, in_ap=in_ap, remote_sem=rsem, local_sem=sem.snt, pid=pid, routing_id=rid,
+                     dma_engine_mask=m)
 
     sy.dma_start(T.qs[:], T.q[:]).then_inc(sem.ql, 16)
     if core in feeds:
@@ -214,18 +234,32 @@ def _rank(g, core, T, topo, job, home, feeds):
         ve.memset(T.va[:, VW + 128:2 * VW], 1.0).then_inc(sem.on, 1)
     ve.memset(T.mask[P, 0:64], 200.0).then_inc(sem.i0, 1)
     g.wait_ge(sem.ql, 16)
-    m, sent = _q_engines(topo, core, w)
-    rid, pid, _ = topo.addr(w)
-    g.remote_dma(out_ap=T.qown[:, 64 * h:64 * h + 64], in_ap=T.qs[:], remote_sem=sem.qa, local_sem=sem.snt, pid=pid,
-                 routing_id=rid, dma_engine_mask=m)
+    if topo.may_write(core, partner):
+        m1, m2, n = _halves(topo, core, [w, partner])
+        tr = [RemoteDMATransfer(dst_ids=[DstId(rid=topo.addr(d)[0], pnc=topo.addr(d)[1])], dma_engine_mask=m,
+                                remote_sem=s, srcs=[T.qs[:]], dsts=[o], alu_op=0)
+              for d, m, s, o in ((partner, m1, sem.qf, T.qfar[:, C]), (w, m2, sem.qa, T.qown[:, C]))]
+        g.remote_dma_fused(tr, local_sem=sem.snt)
+        sent = 2 * n
+        mask_call()
+        if not topo.may_write(other, partner):
+            g.wait_ge(sem.qr, _engines(topo, other, [core, w], NQ)[1])
+            m, n = _engines(topo, core, [partner], NF)
+            send(partner, T.qfar[:, CO], T.qx[:], sem.qf, m)
+            sent += n
+    else:
+        m, n = _engines(topo, core, [other, w], NQ)
+        send(other, T.qx[:], T.qs[:], sem.qr, m)
+        send(w, T.qown[:, C], T.qs[:], sem.qa, m)
+        sent = 2 * n
     if core in feeds:
         g.wait_ge(sem.kl, 16)
         sent += _fan(g, T, topo, core, feeds[core], T.kb[:], T.kb[:], sem.ka, NKV)
         g.wait_ge(sem.vl, 32)
         g.wait_ge(sem.on, 2)
         sent += _fan(g, T, topo, core, feeds[core], T.va[:], T.va[:], sem.va, NKV)
-    g.wait_ge(sem.i0, 1)
-    g.affine_select(T.mask[P, 0:64], T.mask[P, 0:64], [[-1, 64]], A.is_equal, -200.0, 0, 1).then_inc(sem.i1, 1)
+    if not topo.may_write(core, partner):
+        mask_call()
     se.wait_ge(sem.i1, 1)
     se.activation(T.ident[P, 0:64], T.mask[P, 0:64], F.Sigmoid).then_inc(sem.i2, 1)
     ve.wait_ge(sem.i2, 1)
@@ -235,19 +269,19 @@ def _rank(g, core, T, topo, job, home, feeds):
     n_a = _engines(topo, w, job[w][1], NR)[1]
     n_b = _engines(topo, partner, job[partner][2], NR)[1]
     ve.wait_ge(sem.i3, 1)
-    ve.wait_ge(sem.resa, n_a)
-    ve.tensor_scalar(T.mn[P, :], T.off[P, :], T.pa[P, 130:131], None, A.add).then_inc(sem.c1, 1)
-    ve.tensor_scalar(T.ma[P, :], T.off[P, :], T.pa[P, 129:130], None, A.add).then_inc(sem.c1, 1)
+    ve.wait_ge(sem.sha, n_a)
+    ve.tensor_scalar(T.ma[P, :], T.off[P, :], T.sa[P, 0:1], None, A.add).then_inc(sem.c1, 1)
+    ve.tensor_scalar(T.mn[P, :], T.off[P, :], T.sa[P, 1:2], None, A.add).then_inc(sem.c1, 1)
     se.wait_ge(sem.c1, 2)
-    se.wait_ge(sem.resb, n_b)
-    se.activation(T.db[P, :], T.mn[P, :], F.Sigmoid, bias=T.pb[P, 129:130]).then_inc(sem.c2, 1)
-    se.activation(T.da[P, :], T.ma[P, :], F.Sigmoid, bias=T.pb[P, 130:131]).then_inc(sem.c3, 1)
-    te.wait_ge(sem.resa, n_a)
-    te.wait_ge(sem.resb, n_b)
-    te.wait_ge(sem.c2, 1)
-    te.matmul(T.o0[0:64, 0:129], T.db[P, :], T.pb[P, 0:129], True, False)
+    se.wait_ge(sem.shb, n_b)
+    se.activation(T.da[P, :], T.ma[P, :], F.Sigmoid, bias=T.sb[P, 1:2]).then_inc(sem.c3, 1)
+    se.activation(T.db[P, :], T.mn[P, :], F.Sigmoid, bias=T.sb[P, 0:1]).then_inc(sem.c2, 1)
     te.wait_ge(sem.c3, 1)
-    te.matmul(T.o0[0:64, 0:129], T.da[P, :], T.pa[P, 0:129], False, True).then_inc(sem.c5, 1)
+    te.wait_ge(sem.resa, n_a)
+    te.matmul(T.o0[0:64, 0:129], T.da[P, :], T.pa[P, :], True, False)
+    te.wait_ge(sem.c2, 1)
+    te.wait_ge(sem.resb, n_b)
+    te.matmul(T.o0[0:64, 0:129], T.db[P, :], T.pb[P, :], False, True).then_inc(sem.c5, 1)
     ve.wait_ge(sem.c5, 1)
     ve.reciprocal(T.rr[0:64, :], T.o0[0:64, 128:129]).then_inc(sem.c8, 1)
     ve.wait_ge(sem.c8, 1)

import math
from concourse.bass import DstId, RemoteDMATransfer
from concourse.mybir import AluOpType, AxisListType, ActivationFunctionType

NQ = 4
NF = 8
NR = 8
NKV = 16

LOW = -1.0e29
OFF = 1.0e9
VW = 136
RW = 129

SCRATCH = {
    "qs": ("sbuf", [128, 64], "bfloat16"),
    "qx": ("sbuf", [128, 64], "bfloat16"),
    "qown": ("sbuf", [128, 128], "bfloat16"),
    "qfar": ("sbuf", [128, 128], "bfloat16"),
    "kb": ("sbuf", [128, 256], "bfloat16"),
    "va": ("sbuf", [128, 2 * VW], "bfloat16"),
    "mask": ("sbuf", [128, 128], "float32"),
    "ident": ("sbuf", [128, 128], "bfloat16"),
    "nid": ("sbuf", [128, 128], "bfloat16"),
    "low": ("sbuf", [128, 384], "bfloat16"),
    "mb0": ("sbuf", [128, 384], "bfloat16"),
    "mb1": ("sbuf", [128, 384], "bfloat16"),
    "p0": ("sbuf", [128, 256], "bfloat16"),
    "p1": ("sbuf", [128, 256], "bfloat16"),
    "sh0": ("sbuf", [128, 2], "bfloat16"),
    "sh1": ("sbuf", [128, 2], "bfloat16"),
    "res0": ("sbuf", [128, RW], "bfloat16"),
    "res1": ("sbuf", [128, RW], "bfloat16"),
    "sa": ("sbuf", [128, 2], "bfloat16"),
    "sb": ("sbuf", [128, 2], "bfloat16"),
    "pa": ("sbuf", [128, RW], "bfloat16"),
    "pb": ("sbuf", [128, RW], "bfloat16"),
    "off": ("sbuf", [128, 64], "float32"),
    "ma": ("sbuf", [128, 64], "float32"),
    "mn": ("sbuf", [128, 64], "float32"),
    "da": ("sbuf", [128, 64], "bfloat16"),
    "db": ("sbuf", [128, 64], "bfloat16"),
    "rr": ("sbuf", [128, 1], "float32"),
    "yb": ("sbuf", [128, 128], "bfloat16"),
    "s0": ("psum", [128, 512], "float32"),
    "s1": ("psum", [128, 512], "float32"),
    "ta0": ("psum", [128, 512], "float32"),
    "tb0": ("psum", [128, 512], "float32"),
    "ta1": ("psum", [128, 512], "float32"),
    "tb1": ("psum", [128, 512], "float32"),
    "o0": ("psum", [128, 512], "float32"),
    "o1": ("psum", [128, 512], "float32"),
}

_BATCH_SEMS = ["sS", "sM", "sTa", "sTb", "sPa", "sPb", "sO", "sL", "sR"]
SEMAPHORES = (["ql", "kl", "vl", "on", "snt", "qa", "qf", "qr", "ka", "va", "sha", "shb", "resa", "resb", "i0", "i1",
               "i2", "i3", "i4", "i5", "st", "c1", "c2", "c3", "c5", "c8", "c9"]
              + [n + str(b) for b in (0, 1) for n in _BATCH_SEMS])


def _engines(topo, src, dsts, n):
    allowed = topo.mask(src, dsts[0])
    for d in dsts[1:]:
        allowed &= topo.mask(src, d)
    bits = [e for e in range(16) if (allowed >> e) & 1]
    n = min(n, len(bits))
    m = 0
    for e in bits[::len(bits) // n][:n]:
        m |= 1 << e
    return m, n


def _halves(topo, src, dsts):
    m, n = _engines(topo, src, dsts, 2 * NQ)
    bits = [e for e in range(16) if (m >> e) & 1]
    return sum(1 << e for e in bits[0::2]), sum(1 << e for e in bits[1::2]), n // 2


def _plan(T, topo):
    cores = list(T.cores)
    mem = [cores[j] for j in T.tables["MEM"]]
    every = range(topo.CHIPS * topo.CORES_PER_CHIP)
    workers, ranks = [], []
    for s in (0, 1):
        ch = topo.chip(mem[s])
        w = [c for c in every if topo.chip(c) == ch and c not in cores and topo.may_write(c, mem[1 - s])]
        r = [c for c in cores if topo.chip(c) == ch or topo.same_plane(topo.chip(c), ch)]
        workers.append({d: [c for c in w if topo.die(c) == d] for d in (0, 1)})
        ranks.append({d: [c for c in r if topo.die(c) == d] for d in (0, 1)})
    job = {}
    home = {}
    for s in (0, 1):
        for d in (0, 1):
            for i, w in enumerate(workers[s][d]):
                job[w] = (workers[1 - s][d][i], ranks[s][d][2 * i:2 * i + 2], ranks[1 - s][d][2 * i:2 * i + 2])
                for h, c in enumerate(ranks[s][d][2 * i:2 * i + 2]):
                    home[c] = (w, h)
    feeds = {mem[s]: workers[s][0] + workers[s][1] for s in (0, 1)}
    return job, home, feeds


def _q_counts(topo, pair, w, partner):
    at_w = at_p = 0
    for i, c in enumerate(pair):
        if topo.may_write(c, partner):
            n = _halves(topo, c, [w, partner])[2]
            at_w += n
            at_p += n
        else:
            at_w += _engines(topo, c, [pair[1 - i], w], NQ)[1]
            at_p += _engines(topo, pair[1 - i], [partner], NF)[1]
    return at_w, at_p


def _fan(g, T, topo, core, dsts, src, dst, sem, n):
    m, n = _engines(topo, core, dsts, n)
    ids = [DstId(rid=topo.addr(c)[0], pnc=topo.addr(c)[1]) for c in dsts]
    g.remote_dma_fused([RemoteDMATransfer(dst_ids=ids, dma_engine_mask=m, remote_sem=sem, srcs=[src],
                                          dsts=[dst for _ in dsts], alu_op=0)], local_sem=T.sem.snt)
    return n


def _worker(g, core, T, topo, job):
    partner, own, far = job[core]
    sem = T.sem
    A, F = AluOpType, ActivationFunctionType
    te, ve, se = g.tensor, g.vector, g.scalar

    ve.memset(T.mask[:], 0.0).then_inc(sem.i0, 1)
    ve.memset(T.low[:], LOW).then_inc(sem.i5, 1)
    ve.memset(T.s0[:, 256:384], LOW).then_inc(sem.i4, 1)
    ve.memset(T.s1[:, 256:384], LOW).then_inc(sem.i4, 1)
    g.wait_ge(sem.i0, 1)
    g.affine_select(T.mask[:], T.mask[:], [[-1, 128]], A.is_equal, -200.0, 0, 1).then_inc(sem.i1, 1)
    se.wait_ge(sem.i1, 1)
    se.activation(T.ident[:], T.mask[:], F.Exp).then_inc(sem.i2, 1)
    ve.wait_ge(sem.i2, 1)
    ve.tensor_scalar(T.nid[:], T.ident[:], -1.0, None, A.mult).then_inc(sem.i3, 1)
    ve.wait_ge(sem.i5, 1)
    ve.wait_ge(sem.i4, 2)

    q_own = _q_counts(topo, own, core, partner)[0]
    q_far = _q_counts(topo, far, partner, core)[1]
    sent = [0]

    def S(n, b):
        return sem[n + str(b)]

    def scores(b):
        q, s = (T.qown, T.qfar)[b], T["s%d" % b]
        if b == 0:
            te.wait_ge(sem.qa, q_own)
            te.wait_ge(sem.ka, NKV)
            te.wait_ge(sem.i4, 2)
        else:
            te.wait_ge(sem.qf, q_far)
        te.matmul(s[:, 0:256], q[:], T.kb[:], True, True).then_inc(S("sS", b), 1)
        te.matmul(T["ta%d" % b][:, 0:128], T.kb[:, 0:128], q[:], True, False)
        te.matmul(T["tb%d" % b][:, 0:128], T.kb[:, 128:256], q[:], True, False)

    def shift(b):
        s, mb, sh = T["s%d" % b], T["mb%d" % b], T["sh%d" % b]
        ve.wait_ge(S("sS", b), 1)
        ve.tensor_tensor_scan(mb[:], s[:, 0:384], T.low[:], LOW, A.max, A.max).then_inc(S("sM", b), 1)
        ve.wait_ge(S("sM", b), 1)
        ve.tensor_copy(sh[:, 0:1], mb[:, 383:384]).then_inc(S("sL", b), 1)
        ve.tensor_scalar(sh[:, 1:2], mb[:, 383:384], -1.0, None, A.mult).then_inc(S("sL", b), 1)
        g.wait_ge(S("sL", b), 2)
        sent[0] += _fan(g, T, topo, core, (own, far)[b], sh[:], (T.sa, T.sb)[b][:], (sem.sha, sem.shb)[b], NR)

    def shifted(b):
        mb = T["mb%d" % b]
        if b == 0:
            te.wait_ge(sem.i3, 1)
        te.wait_ge(S("sM", b), 1)
        te.matmul(T["ta%d" % b][:, 0:128], mb[:, 256:384], T.nid[:], False, True).then_inc(S("sTa", b), 1)
        te.matmul(T["tb%d" % b][:, 0:128], mb[:, 256:384], T.nid[:], False, True).then_inc(S("sTb", b), 1)

    def weights(b):
        p = T["p%d" % b]
        se.wait_ge(S("sTa", b), 1)
        se.activation(p[:, 0:128], T["ta%d" % b][:, 0:128], F.Exp).then_inc(S("sPa", b), 1)
        se.wait_ge(S("sTb", b), 1)
        se.activation(p[:, 128:256], T["tb%d" % b][:, 0:128], F.Exp).then_inc(S("sPb", b), 1)

    def values(b):
        p, o = T["p%d" % b], T["o%d" % b]
        if b == 0:
            te.wait_ge(sem.va, NKV)
        te.wait_ge(S("sPa", b), 1)
        te.matmul(o[:, 0:129], p[:, 0:128], T.va[:, 0:129], True, False)
        te.wait_ge(S("sPb", b), 1)
        te.matmul(o[:, 0:129], p[:, 128:256], T.va[:, VW:VW + 129], False, True).then_inc(S("sO", b), 1)

    def result(b):
        res = T["res%d" % b]
        ve.wait_ge(S("sO", b), 1)
        ve.tensor_copy(res[:], T["o%d" % b][:, 0:129]).then_inc(S("sR", b), 1)
        g.wait_ge(S("sR", b), 1)
        sent[0] += _fan(g, T, topo, core, (own, far)[b], res[:], (T.pa, T.pb)[b][:], (sem.resa, sem.resb)[b], NR)

    for stage in (scores, shift, shifted, weights, values, result):
        stage(0)
        stage(1)
    g.wait_ge(sem.snt, sent[0])


def _rank(g, core, T, topo, job, home, feeds):
    sem = T.sem
    A, F = AluOpType, ActivationFunctionType
    te, ve, se, sy = g.tensor, g.vector, g.scalar, g.sync
    w, h = home[core]
    partner, pair = job[w][0], job[w][1]
    other = pair[1 - h]
    P = slice(64 * h, 64 * h + 64)
    C = slice(64 * h, 64 * h + 64)
    CO = slice(64 * (1 - h), 64 * (1 - h) + 64)

    def mask_call():
        g.wait_ge(sem.i0, 1)
        g.affine_select(T.mask[P, 0:64], T.mask[P, 0:64], [[-1, 64]], A.is_equal, -200.0, 0, 1).then_inc(sem.i1, 1)

    def send(dst_core, out_ap, in_ap, rsem, m):
        rid, pid, _ = topo.addr(dst_core)
        g.remote_dma(out_ap=out_ap, in_ap=in_ap, remote_sem=rsem, local_sem=sem.snt, pid=pid, routing_id=rid,
                     dma_engine_mask=m)

    sy.dma_start(T.qs[:], T.q[:]).then_inc(sem.ql, 16)
    if core in feeds:
        se.dma_start(T.kb[:], T.k[:]).then_inc(sem.kl, 16)
        sy.dma_start(T.va[:, 0:128], T.v[:, 0:128]).then_inc(sem.vl, 16)
        se.dma_start(T.va[:, VW:VW + 128], T.v[:, 128:256]).then_inc(sem.vl, 16)
        ve.memset(T.va[:, 128:VW], 1.0).then_inc(sem.on, 1)
        ve.memset(T.va[:, VW + 128:2 * VW], 1.0).then_inc(sem.on, 1)
    ve.memset(T.mask[P, 0:64], 200.0).then_inc(sem.i0, 1)
    g.wait_ge(sem.ql, 16)
    if topo.may_write(core, partner):
        m1, m2, n = _halves(topo, core, [w, partner])
        tr = [RemoteDMATransfer(dst_ids=[DstId(rid=topo.addr(d)[0], pnc=topo.addr(d)[1])], dma_engine_mask=m,
                                remote_sem=s, srcs=[T.qs[:]], dsts=[o], alu_op=0)
              for d, m, s, o in ((partner, m1, sem.qf, T.qfar[:, C]), (w, m2, sem.qa, T.qown[:, C]))]
        g.remote_dma_fused(tr, local_sem=sem.snt)
        sent = 2 * n
        mask_call()
        if not topo.may_write(other, partner):
            g.wait_ge(sem.qr, _engines(topo, other, [core, w], NQ)[1])
            m, n = _engines(topo, core, [partner], NF)
            send(partner, T.qfar[:, CO], T.qx[:], sem.qf, m)
            sent += n
    else:
        m, n = _engines(topo, core, [other, w], NQ)
        send(other, T.qx[:], T.qs[:], sem.qr, m)
        send(w, T.qown[:, C], T.qs[:], sem.qa, m)
        sent = 2 * n
    if core in feeds:
        g.wait_ge(sem.kl, 16)
        sent += _fan(g, T, topo, core, feeds[core], T.kb[:], T.kb[:], sem.ka, NKV)
        g.wait_ge(sem.vl, 32)
        g.wait_ge(sem.on, 2)
        sent += _fan(g, T, topo, core, feeds[core], T.va[:], T.va[:], sem.va, NKV)
    if not topo.may_write(core, partner):
        mask_call()
    se.wait_ge(sem.i1, 1)
    se.activation(T.ident[P, 0:64], T.mask[P, 0:64], F.Sigmoid).then_inc(sem.i2, 1)
    ve.wait_ge(sem.i2, 1)
    ve.tensor_scalar(T.off[P, :], T.ident[P, 0:64], 1.0, OFF, A.subtract, A.mult).then_inc(sem.i3, 1)
    g.wait_ge(sem.snt, sent)

    n_a = _engines(topo, w, job[w][1], NR)[1]
    n_b = _engines(topo, partner, job[partner][2], NR)[1]
    ve.wait_ge(sem.i3, 1)
    ve.wait_ge(sem.sha, n_a)
    ve.tensor_scalar(T.ma[P, :], T.off[P, :], T.sa[P, 0:1], None, A.add).then_inc(sem.c1, 1)
    ve.tensor_scalar(T.mn[P, :], T.off[P, :], T.sa[P, 1:2], None, A.add).then_inc(sem.c1, 1)
    se.wait_ge(sem.c1, 2)
    se.wait_ge(sem.shb, n_b)
    se.activation(T.da[P, :], T.ma[P, :], F.Sigmoid, bias=T.sb[P, 1:2]).then_inc(sem.c3, 1)
    se.activation(T.db[P, :], T.mn[P, :], F.Sigmoid, bias=T.sb[P, 0:1]).then_inc(sem.c2, 1)
    te.wait_ge(sem.c3, 1)
    te.wait_ge(sem.resa, n_a)
    te.matmul(T.o0[0:64, 0:129], T.da[P, :], T.pa[P, :], True, False)
    te.wait_ge(sem.c2, 1)
    te.wait_ge(sem.resb, n_b)
    te.matmul(T.o0[0:64, 0:129], T.db[P, :], T.pb[P, :], False, True).then_inc(sem.c5, 1)
    ve.wait_ge(sem.c5, 1)
    ve.reciprocal(T.rr[0:64, :], T.o0[0:64, 128:129]).then_inc(sem.c8, 1)
    ve.wait_ge(sem.c8, 1)
    ve.tensor_scalar(T.yb[0:64, :], T.o0[0:64, 0:128], T.rr[0:64, :], None, A.mult).then_inc(sem.c9, 1)
    sy.wait_ge(sem.c9, 1)
    sy.dma_start(T.y[:], T.yb[0:64, :]).then_inc(sem.st, 16)
    sy.wait_ge(sem.st, 16)


def rank_program(g, core, T, topo):
    job, home, feeds = _plan(T, topo)
    if core in job:
        _worker(g, core, T, topo, job)
    elif T.rank_of(core) is not None:
        _rank(g, core, T, topo, job, home, feeds)
